import numpy as np
import ml_dtypes


def mxq(x, axis, fmt="e4m3"):
    dtype, down = {"e4m3": (ml_dtypes.float8_e4m3fn, 7), "e5m2": (ml_dtypes.float8_e5m2, 14)}[fmt]
    v = np.moveaxis(np.asarray(x, np.float32).astype(ml_dtypes.bfloat16).astype(np.float64), axis, -1)
    blocks = v.reshape(v.shape[:-1] + (-1, 32))
    amax = np.abs(blocks).max(-1, keepdims=True)
    byte = np.maximum(np.where(amax > 0, np.frexp(amax)[1] - 1 + 127, 0) - down, 1)
    scale = np.exp2(byte - 127.0)
    codes = (blocks / scale).astype(np.float32).astype(dtype).astype(np.float64)
    return np.moveaxis((codes * scale).reshape(v.shape), -1, axis)


WIDE = False


def mx_kscale(k):
    if not WIDE:
        return np.ones(k)
    levels = np.array([10, -10, 5, -5, 0])
    if k % 512:
        return np.exp2(np.random.permutation(np.resize(levels, k // 32))).repeat(32)
    a = np.empty((k // 512, 16))
    for p in range(k // 512):
        a[p, :8] = np.random.permutation(np.resize(levels, 8))
        for g in range(8):
            far = levels[np.abs(levels - a[p, g]) >= 10]
            a[p, g + 8] = far[np.random.randint(len(far))]
    return np.exp2(a.ravel()).repeat(32)


def f64(x):
    return np.asarray(x).astype(np.float64)


def striped(idx):
    return np.tile(idx.reshape(-1, 16).T, (8, 1)).astype(np.uint16)


def unstriped(offs):
    return offs[:16].T.reshape(-1).astype(np.int64)


E2M1 = np.array([0.0, 0.5, 1.0, 1.5, 2.0, 3.0, 4.0, 6.0, -0.0, -0.5, -1.0, -1.5, -2.0, -3.0, -4.0, -6.0])


def pack_weight(w, fmt):
    k, n = w.shape
    w = f64(np.asarray(w, np.float32).astype(ml_dtypes.bfloat16)).reshape(k // 32, 32, n)
    amax = np.abs(w).max(1)
    if fmt == "e4m3":
        byte = np.frexp(amax)[1] - 1 + 127 - 7
    else:
        mant, ex = np.frexp(amax / 6.0)
        byte = np.where(mant > 0.5, ex, ex - 1) + 127
    byte = np.clip(np.where(amax > 0, byte, 1), 1, 254)
    scaled = (w * np.exp2(127.0 - byte)[:, None, :]).reshape(k, n).astype(np.float32)
    by_word = np.ascontiguousarray(scaled.reshape(k // 512, 128, 4, n).transpose(0, 1, 3, 2))
    if fmt == "e4m3":
        words = by_word.astype(ml_dtypes.float8_e4m3fn).view(np.uint8)
    else:
        c = by_word.astype(ml_dtypes.float4_e2m1fn).view(np.uint8) & 0xF
        words = (c[..., 0::2] | (c[..., 1::2] << 4)).reshape(k // 512, 128, 2 * n)
    return np.ascontiguousarray(words), np.ascontiguousarray(byte.astype(np.uint8).reshape(k // 512, 16, n))


def unpack_weight(words, scales, fmt):
    g, _, n = scales.shape
    words = np.ascontiguousarray(words).reshape(g, 128, n, -1)
    if fmt == "e4m3":
        vals = words.view(ml_dtypes.float8_e4m3fn).astype(np.float64)
    else:
        nib = np.empty((g, 128, n, 4), np.uint8)
        nib[..., 0::2] = words & 0xF
        nib[..., 1::2] = words >> 4
        vals = E2M1[nib]
    vals = vals * np.repeat(np.exp2(scales.astype(np.float64) - 127.0), 8, axis=1)[..., None]
    return vals.transpose(0, 1, 3, 2).reshape(g * 512, n)


def gelu(v):
    return 0.5 * v * (1.0 + np.tanh(np.sqrt(2.0 / np.pi) * (v + 0.044715 * v**3)))


def striped8(idx):
    return np.concatenate([v.reshape(-1, 16).T for v in idx]).astype(np.uint16)


def unstriped8(offs):
    return np.stack([offs[16 * g:16 * g + 16].T.reshape(-1) for g in range(8)]).astype(np.int64)


def heads(h, wgt, idx8):
    r = np.arange(h.shape[0])
    return wgt[r // 4 % 128] * h[r[:, None], idx8[r % 512 // 64]]


def put_heads(h, wgs, idx8, t2):
    r = np.arange(h.shape[0])
    page = np.zeros((h.shape[0], t2))
    page[r[:, None], idx8[r % 512 // 64]] = wgs[r // 4 % 128] * h
    return page


K, H, N, T, S, P, T2 = 1024, 512, 1024, 4096, 1024, 512, 1024

def setup_inputs():
    n = np.random.standard_normal
    s = mx_kscale(K)[:, None]
    u = mx_kscale(H)[:, None]
    d = {}
    d["tab_words"], d["tab_scales"] = pack_weight(n((K, T)) * s, "e4m3")
    d["offs"] = striped(np.random.permutation(T)[:S])
    d["w1_words"], d["w1_scales"] = pack_weight(1.2 * n((K, H)) / s * u.T / K ** 0.5, "e2m1")
    d["w2"] = (0.54 * n((K, H)) / s / K ** 0.5).astype(np.float32)
    d["w3"] = (0.7 * n((K, H)) / s * u.T / K ** 0.5).astype(np.float32)
    d["offs2"] = striped8(np.stack([np.random.permutation(S)[:P] for _ in range(8)]))
    d["wgt"] = np.repeat(np.random.uniform(0.5, 2.0, (8, P)), 16, axis=0).astype(np.float32)
    d["lim"] = (np.random.uniform(0.2, 1.2, H) * u[:, 0]).astype(np.float32)
    d["w4_words"], d["w4_scales"] = pack_weight(n((H, N)) / u / H ** 0.5, "e4m3")
    d["offs3"] = striped8(np.stack([np.random.permutation(T2)[:P] for _ in range(8)]))
    d["wgo"] = np.repeat(np.random.uniform(0.5, 2.0, (8, P)), 16, axis=0).astype(np.float32)
    return d

def reference(tab_words, tab_scales, offs, w1_words, w1_scales, w2, w3, offs2, wgt, lim, w4_words, w4_scales, offs3, wgo):
    v = unpack_weight(tab_words, tab_scales, "e4m3")[:, unstriped(offs)]
    w1 = unpack_weight(w1_words, w1_scales, "e2m1")
    a = w1.T @ v
    b = mxq(f64(w2), 0, "e4m3").T @ v
    e = mxq(f64(w3), 0, "e4m3").T @ v
    h = a * np.cos(b) - e
    x = heads(h, f64(wgt), unstriped8(offs2))
    z = mxq(np.minimum(x, f64(lim)[:, None]), 0, "e4m3")
    w4 = unpack_weight(w4_words, w4_scales, "e4m3")
    y = np.exp(-np.abs(w4.T @ z))
    return put_heads(y, f64(wgo), unstriped8(offs3), T2)

@@ -1,0 +1,236 @@
+import math
+from contextlib import ExitStack
+
+import concourse.mybir as mybir
+
+K, H, N, T, S, PICK, T2 = 1024, 512, 1024, 4096, 1024, 512, 1024
+FLOPS = 2 * (3 * K * H * S + H * N * PICK)
+
+F32 = mybir.dt.float32
+BF16 = mybir.dt.bfloat16
+I32 = mybir.dt.int32
+U32 = mybir.dt.uint32
+U16 = mybir.dt.uint16
+U8 = mybir.dt.uint8
+FP8X4 = mybir.dt.float8_e4m3fn_x4
+FP4X4 = mybir.dt.float4_e2m1fn_x4
+ALU = mybir.AluOpType
+ACT = mybir.ActivationFunctionType
+
+P = 128
+PACK = 4
+PASSES = K // (P * PACK)
+BANK = 512
+PAGES = 3
+
+
+def tile_list_herd_calm_slots_kernel(
+    tc, tab_words, tab_scales, offs, w1_words, w1_scales, w2, w3, offs2, wgt, lim, w4_words, w4_scales, offs3, wgo, out
+):
+    nc = tc.nc
+    with ExitStack() as ctx:
+        keep = ctx.enter_context(tc.tile_pool(name="keep", bufs=1))
+        work = ctx.enter_context(tc.tile_pool(name="work", bufs=3))
+        psum = ctx.enter_context(tc.psum_pool(name="psum", bufs=2))
+
+        def held(shape, dtype, name):
+            return keep.tile(shape, dtype, name=name, align_bytes=64)
+
+        list1 = keep.tile([P, S // 16], U16, name="list1")
+        list2 = keep.tile([P, PICK // 16], U16, name="list2")
+        list3 = keep.tile([P, PICK // 16], U16, name="list3")
+
+        tab_s = held([P, T], U8, "tab_s")
+        tab_w = [held([P, T], I32, "tab_w%d" % a) for a in range(PASSES)]
+        w1s_raw = held([P, PASSES, H], U8, "w1s_raw")
+        w4s_raw = held([P, N], U8, "w4s_raw")
+        v_s1 = held([P, S], U8, "v_s1")
+        pages = [held([P, T2], F32, "page%d" % g) for g in range(PAGES)]
+        warm = held([P, 2], F32, "warm")
+
+        nc.vector.memset(tab_s[:].bitcast(I32), 0)
+        nc.vector.memset(w1s_raw[:].rearrange("p a c -> p (a c)").bitcast(I32), 0)
+        nc.vector.memset(warm[:, 0:1], 0.0)
+        nc.scalar.activation(warm[:, 1:2], warm[:, 0:1], ACT.Sin)
+        nc.vector.memset(v_s1[:].bitcast(I32), 0)
+        nc.vector.memset(w4s_raw[:].bitcast(I32), 0)
+        for page in pages:
+            nc.vector.memset(page[:], 0.0)
+
+        def load_table(a):
+            nc.sync.dma_start(tab_w[a][:], tab_words[a].rearrange("p t i -> p (t i)").bitcast(I32))
+
+        def load_weight(w, a, lo, hi, name):
+            raw = held([P, PACK, hi - lo], F32, name)
+            nc.sync.dma_start(raw[:], w[512 * a : 512 * (a + 1), lo:hi].rearrange("(p j) c -> p j c", j=PACK))
+            return raw
+
+        load_table(0)
+        nc.sync.dma_start(list1[:], offs)
+        for q in range(4):
+            nc.gpsimd.dma_start(tab_s[:].bitcast(I32)[32 * q : 32 * q + 8, :], tab_scales[:, 4 * q : 4 * q + 4, :].bitcast(I32))
+        w2_raw0 = load_weight(w2, 0, 0, H, "w2_raw0")
+        w1w_raw = held([P, PASSES, 2 * H], U8, "w1w_raw")
+        nc.sync.dma_start(w1w_raw[:].bitcast(I32), w1_words.rearrange("a p c -> p a c").bitcast(I32))
+        load_table(1)
+        w2_raw1 = [load_weight(w2, 1, 256 * u, 256 * (u + 1), "w2_raw1%d" % u) for u in range(2)]
+        w3_raw = [[load_weight(w3, a, 256 * u, 256 * (u + 1), "w3_raw%d%d" % (a, u)) for u in range(2)] for a in range(PASSES)]
+        nc.sync.dma_start(list2[:], offs2)
+        wgt_sb = held([P, PICK], F32, "wgt_sb")
+        nc.sync.dma_start(wgt_sb[:], wgt)
+        lim_sb = held([P, PACK], F32, "lim_sb")
+        nc.sync.dma_start(lim_sb[:], lim.rearrange("(p t) -> p t", t=PACK))
+        w4w_raw = held([P, N], I32, "w4w_raw")
+        nc.sync.dma_start(w4w_raw[:], w4_words[0].rearrange("p c i -> p (c i)").bitcast(I32))
+        nc.sync.dma_start(list3[:], offs3)
+        wgo_sb = held([P, PICK], F32, "wgo_sb")
+        nc.sync.dma_start(wgo_sb[:], wgo)
+        for q in range(4):
+            nc.gpsimd.dma_start(
+                w1s_raw[:].bitcast(I32)[32 * q : 32 * q + 4, :, :],
+                w1_scales[:, 4 * q : 4 * q + 4, :].rearrange("a r c -> r a c").bitcast(I32),
+            )
+
+        v_w = [held([P, S], U32, "v_w%d" % a) for a in range(PASSES)]
+        v_s = held([P, S], U8, "v_s")
+        nc.vector.tensor_copy(v_w[0][:], tab_w[0][:].bitcast(U32).indirect(list1[:]))
+        nc.vector.tensor_copy(v_s[:], tab_s[:].indirect(list1[:]))
+        for q in range(4):
+            nc.gpsimd.dma_start(v_s1[:].bitcast(I32)[32 * q : 32 * q + 4, :], v_s[:].bitcast(I32)[32 * q + 4 : 32 * q + 8, :])
+        for q in range(4):
+            nc.sync.dma_start(w4s_raw[:].bitcast(I32)[32 * q : 32 * q + 4, :], w4_scales[0, 4 * q : 4 * q + 4, :].bitcast(I32))
+
+        def deal(copy, grouped, raw, lo):
+            width = raw.shape[2] // PACK
+            copy(
+                grouped[:].rearrange("p (t m j) -> p m j t", t=PACK, j=PACK)[:, lo : lo + width],
+                raw[:].rearrange("p j (m t) -> p m j t", t=PACK),
+            )
+
+        def quantize(grouped, name):
+            codes = held([P, H], U32, name + "_c")
+            scales = held([P, H], U8, name + "_s")
+            nc.vector.quantize_mx(out=codes[:].bitcast(FP8X4), scales=scales[:], in_=grouped[:])
+            return codes, scales
+
+        w2_g = [held([P, PACK * H], BF16, "w2_g%d" % a) for a in range(PASSES)]
+        w3_g = [held([P, PACK * H], BF16, "w3_g%d" % a) for a in range(PASSES)]
+        deal(nc.scalar.copy, w2_g[0], w2_raw0, 0)
+        w2_q = [quantize(w2_g[0], "w2q0")]
+
+        w1_w = held([P, PASSES, 2 * H], U8, "w1_w")
+        w1_s = held([P, PASSES, H], U8, "w1_s")
+        for a in range(PASSES):
+            nc.vector.tensor_copy(
+                w1_w[:, a, :].rearrange("p (t m b) -> p m t b", t=PACK, b=2),
+                w1w_raw[:, a, :].rearrange("p (m t b) -> p m t b", t=PACK, b=2),
+            )
+        nc.vector.tensor_copy(
+            w1_s[:].rearrange("p a (t m) -> p a m t", t=PACK), w1s_raw[:].rearrange("p a (m t) -> p a m t", t=PACK)
+        )
+
+        nc.vector.tensor_copy(v_w[1][:], tab_w[1][:].bitcast(U32).indirect(list1[:]))
+        deal(nc.scalar.copy, w2_g[1], w2_raw1[0], 0)
+        deal(nc.vector.tensor_copy, w2_g[1], w2_raw1[1], 64)
+        w2_q.append(quantize(w2_g[1], "w2q1"))
+
+        def product(name, codes, scales, dtype, width, t, cols, second_plane):
+            acc = psum.tile([P, BANK], F32, name=name)
+            for a in range(PASSES):
+                nc.tensor.matmul_mx(
+                    out=acc[:],
+                    lhsT=codes[a][:, width * t : width * (t + 1)].bitcast(dtype),
+                    lhsT_scale=scales[a][:, P * t : P * (t + 1)],
+                    rhs=v_w[a][:, cols].bitcast(FP8X4),
+                    rhs_scale=v_s[:, cols] if a == 0 else second_plane[:, cols],
+                    start=(a == 0),
+                    stop=(a == PASSES - 1),
+                )
+            return acc
+
+        def cos_part(t, cols):
+            b = product("b", [q[0] for q in w2_q], [q[1] for q in w2_q], FP8X4, P, t, cols, v_s[4:P])
+            turns = work.tile([P, BANK], F32, name="turns")
+            nc.scalar.activation(turns[:], b[:], ACT.Abs, scale=1.0 / (2.0 * math.pi))
+            whole = work.tile([P, BANK], U32, name="whole")
+            nc.scalar.activation(whole[:], turns[:], ACT.Copy, bias=0.25)
+            frac = work.tile([P, BANK], F32, name="frac")
+            nc.vector.scalar_tensor_tensor(frac[:], turns[:], 0.25, whole[:].bitcast(I32), ALU.add, ALU.subtract)
+            cosb = work.tile([P, BANK], F32, name="cosb")
+            nc.scalar.activation(cosb[:], frac[:], ACT.Sin, scale=2.0 * math.pi)
+            a = product("a", [w1_w[:, s, :] for s in range(PASSES)], [w1_s[:, s, :] for s in range(PASSES)], FP4X4, 2 * P, t, cols, v_s1)
+            acos = work.tile([P, BANK], F32, name="acos", bufs=5)
+            nc.vector.tensor_tensor(acos[:], a[:], cosb[:], ALU.mult)
+            return acos, cosb
+
+        units = [(t, slice(BANK * u, BANK * (u + 1))) for t in range(PACK) for u in range(S // BANK)]
+        first = cos_part(*units[0])
+
+        w3_q = []
+        for a, copy in enumerate((nc.vector.tensor_copy, nc.scalar.copy)):
+            deal(copy, w3_g[a], w3_raw[a][0], 0)
+            deal(copy, w3_g[a], w3_raw[a][1], 64)
+            w3_q.append(quantize(w3_g[a], "w3q%d" % a))
+
+        w4_w = held([P, N], I32, "w4_w")
+        w4_s = held([P, N], U8, "w4_s")
+
+        def deal_w4(b, lo, hi):
+            half = slice(512 * b, 512 * (b + 1))
+            for dealt, raw in ((w4_w, w4w_raw), (w4_s, w4s_raw)):
+                nc.vector.tensor_copy(
+                    dealt[:, half].rearrange("p (i m) -> p m i", i=PACK)[:, :, lo:hi],
+                    raw[:, half].rearrange("p (m i) -> p m i", i=PACK)[:, :, lo:hi],
+                )
+
+        h = [held([P, S], F32, "h%d" % t) for t in range(PACK)]
+        zt = held([P, PACK, PICK], BF16, "zt")
+        z_g = held([P, PICK * PACK], BF16, "z_g")
+
+        def pick(t, lo, hi):
+            x = work.tile([P, hi - lo], F32, name="x")
+            nc.vector.tensor_tensor(x[:], h[t][:].indirect(list2[:, lo // 16 : hi // 16]), wgt_sb[:, lo:hi], ALU.mult)
+            nc.vector.tensor_scalar(zt[:, t, lo:hi], x[:], lim_sb[:, t : t + 1], None, ALU.min)
+
+        def interleave(copy, lo, hi):
+            copy(
+                z_g[:, PACK * lo : PACK * hi].rearrange("p (c i t) -> p c t i", i=4, t=PACK),
+                zt[:, :, lo:hi].rearrange("p t (c i) -> p c t i", i=4),
+            )
+
+        for n, (t, cols) in enumerate(units):
+            acos, cosb = first if n == 0 else cos_part(t, cols)
+            e = product("e", [q[0] for q in w3_q], [q[1] for q in w3_q], FP8X4, P, t, cols, v_s[4:P])
+            nc.vector.tensor_tensor(h[t][:, cols], acos[:], e[:], ALU.subtract)
+            if n % 2 == 1 and t < PACK - 1:
+                pick(t, 0, PICK)
+        nc.scalar.activation(warm[:, 0:1], cosb[:, 0:1], ACT.Exp)
+        deal_w4(0, 0, 1)
+        pick(PACK - 1, 0, PICK // 2)
+        interleave(nc.scalar.copy, 0, PICK // 2)
+        pick(PACK - 1, PICK // 2, PICK)
+        interleave(nc.vector.tensor_copy, PICK // 2, PICK)
+        z_c, z_s = quantize(z_g, "zq")
+        deal_w4(0, 1, PACK)
+        deal_w4(1, 0, PACK)
+
+        out_rows = out.rearrange("(b p i) c -> b i p c", p=P, i=PACK)
+        for g in range(N // P):
+            acc = psum.tile([P, BANK], F32, name="y")
+            cols = slice(P * g, P * (g + 1))
+            nc.tensor.matmul_mx(
+                out=acc[:],
+                lhsT=w4_w[:, cols].bitcast(FP8X4),
+                lhsT_scale=w4_s[:, cols],
+                rhs=z_c[:].bitcast(FP8X4),
+                rhs_scale=z_s[:],
+                start=True,
+                stop=True,
+            )
+            mag = work.tile([P, PICK], F32, name="mag")
+            nc.scalar.activation(mag[:], acc[:], ACT.Abs)
+            y = work.tile([P, PICK], F32, name="ysb")
+            nc.scalar.activation(y[:], mag[:], ACT.Exp, scale=-1.0)
+            page = pages[g % PAGES]
+            nc.vector.tensor_tensor(page[:].indirect(list3[:]), y[:], wgo_sb[:], ALU.mult)
+            nc.sync.dma_start(out_rows[g // PACK, g % PACK], page[:])

@@ -44,15 +44,17 @@ def tile_list_herd_calm_slots_kernel(
         tab_w = [held([P, T], I32, "tab_w%d" % a) for a in range(PASSES)]
         w1s_raw = held([P, PASSES, H], U8, "w1s_raw")
         w4s_raw = held([P, N], U8, "w4s_raw")
-        v_s1 = held([P, S], U8, "v_s1")
+        v_s = [held([P, S], U8, "v_s%d" % a) for a in range(PASSES)]
         pages = [held([P, T2], F32, "page%d" % g) for g in range(PAGES)]
         warm = held([P, 2], F32, "warm")
 
-        nc.vector.memset(tab_s[:].bitcast(I32), 0)
         nc.vector.memset(w1s_raw[:].rearrange("p a c -> p (a c)").bitcast(I32), 0)
+        nc.vector.memset(tab_s[:].bitcast(I32)[32:64, :], 0)
+        nc.vector.memset(tab_s[:].bitcast(I32)[64:128, :], 0)
         nc.vector.memset(warm[:, 0:1], 0.0)
         nc.scalar.activation(warm[:, 1:2], warm[:, 0:1], ACT.Sin)
-        nc.vector.memset(v_s1[:].bitcast(I32), 0)
+        for plane in v_s:
+            nc.vector.memset(plane[:].bitcast(I32), 0)
         nc.vector.memset(w4s_raw[:].bitcast(I32), 0)
         for page in pages:
             nc.vector.memset(page[:], 0.0)
@@ -60,21 +62,38 @@ def tile_list_herd_calm_slots_kernel(
         def load_table(a):
             nc.sync.dma_start(tab_w[a][:], tab_words[a].rearrange("p t i -> p (t i)").bitcast(I32))
 
-        def load_weight(w, a, lo, hi, name):
-            raw = held([P, PACK, hi - lo], F32, name)
-            nc.sync.dma_start(raw[:], w[512 * a : 512 * (a + 1), lo:hi].rearrange("(p j) c -> p j c", j=PACK))
+        def load_weight(w, a, name):
+            raw = held([P, PACK, H], F32, name)
+            nc.sync.dma_start(raw[:], w[512 * a : 512 * (a + 1), :].rearrange("(p j) c -> p j c", j=PACK))
             return raw
 
-        load_table(0)
+        nc.sync.dma_start(tab_s[:].bitcast(I32)[0:32, :], tab_scales.rearrange("a q n -> (a q) n").bitcast(I32))
         nc.sync.dma_start(list1[:], offs)
+        load_table(0)
         for q in range(4):
-            nc.gpsimd.dma_start(tab_s[:].bitcast(I32)[32 * q : 32 * q + 8, :], tab_scales[:, 4 * q : 4 * q + 4, :].bitcast(I32))
-        w2_raw0 = load_weight(w2, 0, 0, H, "w2_raw0")
+            nc.sync.dma_start(
+                w1s_raw[:].bitcast(I32)[32 * q : 32 * q + 4, :, :],
+                w1_scales[:, 4 * q : 4 * q + 4, :].rearrange("a r c -> r a c").bitcast(I32),
+            )
         w1w_raw = held([P, PASSES, 2 * H], U8, "w1w_raw")
         nc.sync.dma_start(w1w_raw[:].bitcast(I32), w1_words.rearrange("a p c -> p a c").bitcast(I32))
+        w2_raw0 = load_weight(w2, 0, "w2_raw0")
         load_table(1)
-        w2_raw1 = [load_weight(w2, 1, 256 * u, 256 * (u + 1), "w2_raw1%d" % u) for u in range(2)]
-        w3_raw = [[load_weight(w3, a, 256 * u, 256 * (u + 1), "w3_raw%d%d" % (a, u)) for u in range(2)] for a in range(PASSES)]
+
+        v_rows = held([P, S], U8, "v_rows")
+        nc.vector.tensor_copy(v_rows[:], tab_s[:].indirect(list1[:]))
+
+        def place_rows(a, q):
+            row = 16 * a + 4 * q
+            nc.sync.dma_start(v_s[a][:].bitcast(I32)[32 * q : 32 * q + 4, :], v_rows[:].bitcast(I32)[row : row + 4, :])
+
+        moves = [(a, q) for a in range(PASSES) for q in range(4)]
+        for a, q in moves[:6]:
+            place_rows(a, q)
+        w2_raw1 = load_weight(w2, 1, "w2_raw1")
+        for a, q in moves[6:]:
+            place_rows(a, q)
+        w3_raw = [load_weight(w3, a, "w3_raw%d" % a) for a in range(PASSES)]
         nc.sync.dma_start(list2[:], offs2)
         wgt_sb = held([P, PICK], F32, "wgt_sb")
         nc.sync.dma_start(wgt_sb[:], wgt)
@@ -86,25 +105,15 @@ def tile_list_herd_calm_slots_kernel(
         wgo_sb = held([P, PICK], F32, "wgo_sb")
         nc.sync.dma_start(wgo_sb[:], wgo)
         for q in range(4):
-            nc.gpsimd.dma_start(
-                w1s_raw[:].bitcast(I32)[32 * q : 32 * q + 4, :, :],
-                w1_scales[:, 4 * q : 4 * q + 4, :].rearrange("a r c -> r a c").bitcast(I32),
-            )
-
-        v_w = [held([P, S], U32, "v_w%d" % a) for a in range(PASSES)]
-        v_s = held([P, S], U8, "v_s")
-        nc.vector.tensor_copy(v_w[0][:], tab_w[0][:].bitcast(U32).indirect(list1[:]))
-        nc.vector.tensor_copy(v_s[:], tab_s[:].indirect(list1[:]))
-        for q in range(4):
-            nc.gpsimd.dma_start(v_s1[:].bitcast(I32)[32 * q : 32 * q + 4, :], v_s[:].bitcast(I32)[32 * q + 4 : 32 * q + 8, :])
-        for q in range(4):
             nc.sync.dma_start(w4s_raw[:].bitcast(I32)[32 * q : 32 * q + 4, :], w4_scales[0, 4 * q : 4 * q + 4, :].bitcast(I32))
 
-        def deal(copy, grouped, raw, lo):
-            width = raw.shape[2] // PACK
+        v_w = [held([P, S], U32, "v_w%d" % a) for a in range(PASSES)]
+        nc.vector.tensor_copy(v_w[0][:], tab_w[0][:].bitcast(U32).indirect(list1[:]))
+
+        def deal(copy, grouped, raw, lo, hi):
             copy(
-                grouped[:].rearrange("p (t m j) -> p m j t", t=PACK, j=PACK)[:, lo : lo + width],
-                raw[:].rearrange("p j (m t) -> p m j t", t=PACK),
+                grouped[:].rearrange("p (t m j) -> p m j t", t=PACK, j=PACK)[:, lo:hi],
+                raw[:].rearrange("p j (m t) -> p m j t", t=PACK)[:, lo:hi],
             )
 
         def quantize(grouped, name):
@@ -115,7 +124,7 @@ def tile_list_herd_calm_slots_kernel(
 
         w2_g = [held([P, PACK * H], BF16, "w2_g%d" % a) for a in range(PASSES)]
         w3_g = [held([P, PACK * H], BF16, "w3_g%d" % a) for a in range(PASSES)]
-        deal(nc.scalar.copy, w2_g[0], w2_raw0, 0)
+        deal(nc.scalar.copy, w2_g[0], w2_raw0, 0, P)
         w2_q = [quantize(w2_g[0], "w2q0")]
 
         w1_w = held([P, PASSES, 2 * H], U8, "w1_w")
@@ -130,11 +139,11 @@ def tile_list_herd_calm_slots_kernel(
         )
 
         nc.vector.tensor_copy(v_w[1][:], tab_w[1][:].bitcast(U32).indirect(list1[:]))
-        deal(nc.scalar.copy, w2_g[1], w2_raw1[0], 0)
-        deal(nc.vector.tensor_copy, w2_g[1], w2_raw1[1], 64)
+        deal(nc.scalar.copy, w2_g[1], w2_raw1, 0, 40)
+        deal(nc.vector.tensor_copy, w2_g[1], w2_raw1, 40, P)
         w2_q.append(quantize(w2_g[1], "w2q1"))
 
-        def product(name, codes, scales, dtype, width, t, cols, second_plane):
+        def product(name, codes, scales, dtype, width, t, cols):
             acc = psum.tile([P, BANK], F32, name=name)
             for a in range(PASSES):
                 nc.tensor.matmul_mx(
@@ -142,14 +151,18 @@ def tile_list_herd_calm_slots_kernel(
                     lhsT=codes[a][:, width * t : width * (t + 1)].bitcast(dtype),
                     lhsT_scale=scales[a][:, P * t : P * (t + 1)],
                     rhs=v_w[a][:, cols].bitcast(FP8X4),
-                    rhs_scale=v_s[:, cols] if a == 0 else second_plane[:, cols],
+                    rhs_scale=v_s[a][:, cols],
                     start=(a == 0),
                     stop=(a == PASSES - 1),
                 )
             return acc
 
-        def cos_part(t, cols):
-            b = product("b", [q[0] for q in w2_q], [q[1] for q in w2_q], FP8X4, P, t, cols, v_s[4:P])
+        units = [(t, slice(BANK * u, BANK * (u + 1))) for t in range(PACK) for u in range(S // BANK)]
+        cosines, scaled = {}, {}
+
+        def cosine(n):
+            t, cols = units[n]
+            b = product("b", [q[0] for q in w2_q], [q[1] for q in w2_q], FP8X4, P, t, cols)
             turns = work.tile([P, BANK], F32, name="turns")
             nc.scalar.activation(turns[:], b[:], ACT.Abs, scale=1.0 / (2.0 * math.pi))
             whole = work.tile([P, BANK], U32, name="whole")
@@ -158,19 +171,19 @@ def tile_list_herd_calm_slots_kernel(
             nc.vector.scalar_tensor_tensor(frac[:], turns[:], 0.25, whole[:].bitcast(I32), ALU.add, ALU.subtract)
             cosb = work.tile([P, BANK], F32, name="cosb")
             nc.scalar.activation(cosb[:], frac[:], ACT.Sin, scale=2.0 * math.pi)
-            a = product("a", [w1_w[:, s, :] for s in range(PASSES)], [w1_s[:, s, :] for s in range(PASSES)], FP4X4, 2 * P, t, cols, v_s1)
+            cosines[n] = cosb
+
+        def modulate(n):
+            t, cols = units[n]
+            a = product("a", [w1_w[:, s, :] for s in range(PASSES)], [w1_s[:, s, :] for s in range(PASSES)], FP4X4, 2 * P, t, cols)
             acos = work.tile([P, BANK], F32, name="acos", bufs=5)
-            nc.vector.tensor_tensor(acos[:], a[:], cosb[:], ALU.mult)
-            return acos, cosb
+            nc.vector.tensor_tensor(acos[:], a[:], cosines[n][:], ALU.mult)
+            scaled[n] = acos
 
-        units = [(t, slice(BANK * u, BANK * (u + 1))) for t in range(PACK) for u in range(S // BANK)]
-        first = cos_part(*units[0])
-
-        w3_q = []
-        for a, copy in enumerate((nc.vector.tensor_copy, nc.scalar.copy)):
-            deal(copy, w3_g[a], w3_raw[a][0], 0)
-            deal(copy, w3_g[a], w3_raw[a][1], 64)
-            w3_q.append(quantize(w3_g[a], "w3q%d" % a))
+        def subtract(n):
+            t, cols = units[n]
+            e = product("e", [q[0] for q in w3_q], [q[1] for q in w3_q], FP8X4, P, t, cols)
+            nc.vector.tensor_tensor(h[t][:, cols], scaled[n][:], e[:], ALU.subtract)
 
         w4_w = held([P, N], I32, "w4_w")
         w4_s = held([P, N], U8, "w4_s")
@@ -190,6 +203,9 @@ def tile_list_herd_calm_slots_kernel(
         def pick(t, lo, hi):
             x = work.tile([P, hi - lo], F32, name="x")
             nc.vector.tensor_tensor(x[:], h[t][:].indirect(list2[:, lo // 16 : hi // 16]), wgt_sb[:, lo:hi], ALU.mult)
+            return x
+
+        def limit(t, x, lo, hi):
             nc.vector.tensor_scalar(zt[:, t, lo:hi], x[:], lim_sb[:, t : t + 1], None, ALU.min)
 
         def interleave(copy, lo, hi):
@@ -198,20 +214,44 @@ def tile_list_herd_calm_slots_kernel(
                 zt[:, :, lo:hi].rearrange("p t (c i) -> p c t i", i=4),
             )
 
-        for n, (t, cols) in enumerate(units):
-            acos, cosb = first if n == 0 else cos_part(t, cols)
-            e = product("e", [q[0] for q in w3_q], [q[1] for q in w3_q], FP8X4, P, t, cols, v_s[4:P])
-            nc.vector.tensor_tensor(h[t][:, cols], acos[:], e[:], ALU.subtract)
-            if n % 2 == 1 and t < PACK - 1:
-                pick(t, 0, PICK)
-        nc.scalar.activation(warm[:, 0:1], cosb[:, 0:1], ACT.Exp)
+        w3_q = []
+        cosine(0)
+        deal(nc.scalar.copy, w3_g[0], w3_raw[0], 0, 32)
+        deal(nc.vector.tensor_copy, w3_g[0], w3_raw[0], 32, P)
+        cosine(1)
+        w3_q.append(quantize(w3_g[0], "w3q0"))
+        modulate(0)
+        deal(nc.scalar.copy, w3_g[1], w3_raw[1], 0, 64)
+        deal(nc.vector.tensor_copy, w3_g[1], w3_raw[1], 64, P)
+        cosine(2)
+        w3_q.append(quantize(w3_g[1], "w3q1"))
+        modulate(1)
+        for n in range(3, len(units) + 3):
+            done = n - 4
+            row_done = done >= 0 and done % 2 == 1
+            if n < len(units):
+                cosine(n)
+            if row_done:
+                x = pick(done // 2, 0, PICK)
+            if n - 1 < len(units):
+                modulate(n - 1)
+            if n - 1 == len(units) - 1:
+                nc.scalar.activation(warm[:, 0:1], cosines[n - 1][:, 0:1], ACT.Exp)
+            subtract(n - 3)
+            if row_done:
+                limit(done // 2, x, 0, PICK)
+        last, mid = PACK - 1, PICK // 2
         deal_w4(0, 0, 1)
-        pick(PACK - 1, 0, PICK // 2)
-        interleave(nc.scalar.copy, 0, PICK // 2)
-        pick(PACK - 1, PICK // 2, PICK)
-        interleave(nc.vector.tensor_copy, PICK // 2, PICK)
+        xa = pick(last, 0, mid)
+        xb = pick(last, mid, PICK)
+        limit(last, xa, 0, mid)
+        interleave(nc.scalar.copy, 0, mid)
+        limit(last, xb, mid, PICK)
+        deal_w4(0, 1, 2)
+        interleave(nc.vector.tensor_copy, mid, PICK)
+        deal_w4(0, 2, 3)
         z_c, z_s = quantize(z_g, "zq")
-        deal_w4(0, 1, PACK)
+        deal_w4(0, 3, 4)
         deal_w4(1, 0, PACK)
 
         out_rows = out.rearrange("(b p i) c -> b i p c", p=P, i=PACK)

import math
from contextlib import ExitStack

import concourse.mybir as mybir

K, H, N, T, S, PICK, T2 = 1024, 512, 1024, 4096, 1024, 512, 1024
FLOPS = 2 * (3 * K * H * S + H * N * PICK)

F32 = mybir.dt.float32
BF16 = mybir.dt.bfloat16
I32 = mybir.dt.int32
U32 = mybir.dt.uint32
U16 = mybir.dt.uint16
U8 = mybir.dt.uint8
FP8X4 = mybir.dt.float8_e4m3fn_x4
FP4X4 = mybir.dt.float4_e2m1fn_x4
ALU = mybir.AluOpType
ACT = mybir.ActivationFunctionType

P = 128
PACK = 4
PASSES = K // (P * PACK)
BANK = 512
PAGES = 3


def tile_list_herd_calm_slots_kernel(
    tc, tab_words, tab_scales, offs, w1_words, w1_scales, w2, w3, offs2, wgt, lim, w4_words, w4_scales, offs3, wgo, out
):
    nc = tc.nc
    with ExitStack() as ctx:
        keep = ctx.enter_context(tc.tile_pool(name="keep", bufs=1))
        work = ctx.enter_context(tc.tile_pool(name="work", bufs=3))
        psum = ctx.enter_context(tc.psum_pool(name="psum", bufs=2))

        def held(shape, dtype, name):
            return keep.tile(shape, dtype, name=name, align_bytes=64)

        list1 = keep.tile([P, S // 16], U16, name="list1")
        list2 = keep.tile([P, PICK // 16], U16, name="list2")
        list3 = keep.tile([P, PICK // 16], U16, name="list3")

        tab_s = held([P, T], U8, "tab_s")
        tab_w = [held([P, T], I32, "tab_w%d" % a) for a in range(PASSES)]
        w1s_raw = held([P, PASSES, H], U8, "w1s_raw")
        w4s_raw = held([P, N], U8, "w4s_raw")
        v_s = [held([P, S], U8, "v_s%d" % a) for a in range(PASSES)]
        pages = [held([P, T2], F32, "page%d" % g) for g in range(PAGES)]
        warm = held([P, 2], F32, "warm")

        nc.vector.memset(w1s_raw[:].rearrange("p a c -> p (a c)").bitcast(I32), 0)
        nc.vector.memset(tab_s[:].bitcast(I32)[32:64, :], 0)
        nc.vector.memset(tab_s[:].bitcast(I32)[64:128, :], 0)
        nc.vector.memset(warm[:, 0:1], 0.0)
        nc.scalar.activation(warm[:, 1:2], warm[:, 0:1], ACT.Sin)
        for plane in v_s:
            nc.vector.memset(plane[:].bitcast(I32), 0)
        nc.vector.memset(w4s_raw[:].bitcast(I32), 0)
        for page in pages:
            nc.vector.memset(page[:], 0.0)

        def load_table(a):
            nc.sync.dma_start(tab_w[a][:], tab_words[a].rearrange("p t i -> p (t i)").bitcast(I32))

        def load_weight(w, a, name):
            raw = held([P, PACK, H], F32, name)
            nc.sync.dma_start(raw[:], w[512 * a : 512 * (a + 1), :].rearrange("(p j) c -> p j c", j=PACK))
            return raw

        nc.sync.dma_start(tab_s[:].bitcast(I32)[0:32, :], tab_scales.rearrange("a q n -> (a q) n").bitcast(I32))
        nc.sync.dma_start(list1[:], offs)
        load_table(0)
        for q in range(4):
            nc.sync.dma_start(
                w1s_raw[:].bitcast(I32)[32 * q : 32 * q + 4, :, :],
                w1_scales[:, 4 * q : 4 * q + 4, :].rearrange("a r c -> r a c").bitcast(I32),
            )
        w1w_raw = held([P, PASSES, 2 * H], U8, "w1w_raw")
        nc.sync.dma_start(w1w_raw[:].bitcast(I32), w1_words.rearrange("a p c -> p a c").bitcast(I32))
        w2_raw0 = load_weight(w2, 0, "w2_raw0")
        load_table(1)

        v_rows = held([P, S], U8, "v_rows")
        nc.vector.tensor_copy(v_rows[:], tab_s[:].indirect(list1[:]))

        def place_rows(a, q):
            row = 16 * a + 4 * q
            nc.sync.dma_start(v_s[a][:].bitcast(I32)[32 * q : 32 * q + 4, :], v_rows[:].bitcast(I32)[row : row + 4, :])

        moves = [(a, q) for a in range(PASSES) for q in range(4)]
        for a, q in moves[:6]:
            place_rows(a, q)
        w2_raw1 = load_weight(w2, 1, "w2_raw1")
        for a, q in moves[6:]:
            place_rows(a, q)
        w3_raw = [load_weight(w3, a, "w3_raw%d" % a) for a in range(PASSES)]
        nc.sync.dma_start(list2[:], offs2)
        wgt_sb = held([P, PICK], F32, "wgt_sb")
        nc.sync.dma_start(wgt_sb[:], wgt)
        lim_sb = held([P, PACK], F32, "lim_sb")
        nc.sync.dma_start(lim_sb[:], lim.rearrange("(p t) -> p t", t=PACK))
        w4w_raw = held([P, N], I32, "w4w_raw")
        nc.sync.dma_start(w4w_raw[:], w4_words[0].rearrange("p c i -> p (c i)").bitcast(I32))
        nc.sync.dma_start(list3[:], offs3)
        wgo_sb = held([P, PICK], F32, "wgo_sb")
        nc.sync.dma_start(wgo_sb[:], wgo)
        for q in range(4):
            nc.sync.dma_start(w4s_raw[:].bitcast(I32)[32 * q : 32 * q + 4, :], w4_scales[0, 4 * q : 4 * q + 4, :].bitcast(I32))

        v_w = [held([P, S], U32, "v_w%d" % a) for a in range(PASSES)]
        nc.vector.tensor_copy(v_w[0][:], tab_w[0][:].bitcast(U32).indirect(list1[:]))

        def deal(copy, grouped, raw, lo, hi):
            copy(
                grouped[:].rearrange("p (t m j) -> p m j t", t=PACK, j=PACK)[:, lo:hi],
                raw[:].rearrange("p j (m t) -> p m j t", t=PACK)[:, lo:hi],
            )

        def quantize(grouped, name):
            codes = held([P, H], U32, name + "_c")
            scales = held([P, H], U8, name + "_s")
            nc.vector.quantize_mx(out=codes[:].bitcast(FP8X4), scales=scales[:], in_=grouped[:])
            return codes, scales

        w2_g = [held([P, PACK * H], BF16, "w2_g%d" % a) for a in range(PASSES)]
        w3_g = [held([P, PACK * H], BF16, "w3_g%d" % a) for a in range(PASSES)]
        deal(nc.scalar.copy, w2_g[0], w2_raw0, 0, P)
        w2_q = [quantize(w2_g[0], "w2q0")]

        w1_w = held([P, PASSES, 2 * H], U8, "w1_w")
        w1_s = held([P, PASSES, H], U8, "w1_s")
        for a in range(PASSES):
            nc.vector.tensor_copy(
                w1_w[:, a, :].rearrange("p (t m b) -> p m t b", t=PACK, b=2),
                w1w_raw[:, a, :].rearrange("p (m t b) -> p m t b", t=PACK, b=2),
            )
        nc.vector.tensor_copy(
            w1_s[:].rearrange("p a (t m) -> p a m t", t=PACK), w1s_raw[:].rearrange("p a (m t) -> p a m t", t=PACK)
        )

        nc.vector.tensor_copy(v_w[1][:], tab_w[1][:].bitcast(U32).indirect(list1[:]))
        deal(nc.scalar.copy, w2_g[1], w2_raw1, 0, 40)
        deal(nc.vector.tensor_copy, w2_g[1], w2_raw1, 40, P)
        w2_q.append(quantize(w2_g[1], "w2q1"))

        def product(name, codes, scales, dtype, width, t, cols):
            acc = psum.tile([P, BANK], F32, name=name)
            for a in range(PASSES):
                nc.tensor.matmul_mx(
                    out=acc[:],
                    lhsT=codes[a][:, width * t : width * (t + 1)].bitcast(dtype),
                    lhsT_scale=scales[a][:, P * t : P * (t + 1)],
                    rhs=v_w[a][:, cols].bitcast(FP8X4),
                    rhs_scale=v_s[a][:, cols],
                    start=(a == 0),
                    stop=(a == PASSES - 1),
                )
            return acc

        units = [(t, slice(BANK * u, BANK * (u + 1))) for t in range(PACK) for u in range(S // BANK)]
        cosines, scaled = {}, {}

        def cosine(n):
            t, cols = units[n]
            b = product("b", [q[0] for q in w2_q], [q[1] for q in w2_q], FP8X4, P, t, cols)
            turns = work.tile([P, BANK], F32, name="turns")
            nc.scalar.activation(turns[:], b[:], ACT.Abs, scale=1.0 / (2.0 * math.pi))
            whole = work.tile([P, BANK], U32, name="whole")
            nc.scalar.activation(whole[:], turns[:], ACT.Copy, bias=0.25)
            frac = work.tile([P, BANK], F32, name="frac")
            nc.vector.scalar_tensor_tensor(frac[:], turns[:], 0.25, whole[:].bitcast(I32), ALU.add, ALU.subtract)
            cosb = work.tile([P, BANK], F32, name="cosb")
            nc.scalar.activation(cosb[:], frac[:], ACT.Sin, scale=2.0 * math.pi)
            cosines[n] = cosb

        def modulate(n):
            t, cols = units[n]
            a = product("a", [w1_w[:, s, :] for s in range(PASSES)], [w1_s[:, s, :] for s in range(PASSES)], FP4X4, 2 * P, t, cols)
            acos = work.tile([P, BANK], F32, name="acos", bufs=5)
            nc.vector.tensor_tensor(acos[:], a[:], cosines[n][:], ALU.mult)
            scaled[n] = acos

        def subtract(n):
            t, cols = units[n]
            e = product("e", [q[0] for q in w3_q], [q[1] for q in w3_q], FP8X4, P, t, cols)
            nc.vector.tensor_tensor(h[t][:, cols], scaled[n][:], e[:], ALU.subtract)

        w4_w = held([P, N], I32, "w4_w")
        w4_s = held([P, N], U8, "w4_s")

        def deal_w4(b, lo, hi):
            half = slice(512 * b, 512 * (b + 1))
            for dealt, raw in ((w4_w, w4w_raw), (w4_s, w4s_raw)):
                nc.vector.tensor_copy(
                    dealt[:, half].rearrange("p (i m) -> p m i", i=PACK)[:, :, lo:hi],
                    raw[:, half].rearrange("p (m i) -> p m i", i=PACK)[:, :, lo:hi],
                )

        h = [held([P, S], F32, "h%d" % t) for t in range(PACK)]
        zt = held([P, PACK, PICK], BF16, "zt")
        z_g = held([P, PICK * PACK], BF16, "z_g")

        def pick(t, lo, hi):
            x = work.tile([P, hi - lo], F32, name="x")
            nc.vector.tensor_tensor(x[:], h[t][:].indirect(list2[:, lo // 16 : hi // 16]), wgt_sb[:, lo:hi], ALU.mult)
            return x

        def limit(t, x, lo, hi):
            nc.vector.tensor_scalar(zt[:, t, lo:hi], x[:], lim_sb[:, t : t + 1], None, ALU.min)

        def interleave(copy, lo, hi):
            copy(
                z_g[:, PACK * lo : PACK * hi].rearrange("p (c i t) -> p c t i", i=4, t=PACK),
                zt[:, :, lo:hi].rearrange("p t (c i) -> p c t i", i=4),
            )

        w3_q = []
        cosine(0)
        deal(nc.scalar.copy, w3_g[0], w3_raw[0], 0, 32)
        deal(nc.vector.tensor_copy, w3_g[0], w3_raw[0], 32, P)
        cosine(1)
        w3_q.append(quantize(w3_g[0], "w3q0"))
        modulate(0)
        deal(nc.scalar.copy, w3_g[1], w3_raw[1], 0, 64)
        deal(nc.vector.tensor_copy, w3_g[1], w3_raw[1], 64, P)
        cosine(2)
        w3_q.append(quantize(w3_g[1], "w3q1"))
        modulate(1)
        for n in range(3, len(units) + 3):
            done = n - 4
            row_done = done >= 0 and done % 2 == 1
            if n < len(units):
                cosine(n)
            if row_done:
                x = pick(done // 2, 0, PICK)
            if n - 1 < len(units):
                modulate(n - 1)
            if n - 1 == len(units) - 1:
                nc.scalar.activation(warm[:, 0:1], cosines[n - 1][:, 0:1], ACT.Exp)
            subtract(n - 3)
            if row_done:
                limit(done // 2, x, 0, PICK)
        last, mid = PACK - 1, PICK // 2
        deal_w4(0, 0, 1)
        xa = pick(last, 0, mid)
        xb = pick(last, mid, PICK)
        limit(last, xa, 0, mid)
        interleave(nc.scalar.copy, 0, mid)
        limit(last, xb, mid, PICK)
        deal_w4(0, 1, 2)
        interleave(nc.vector.tensor_copy, mid, PICK)
        deal_w4(0, 2, 3)
        z_c, z_s = quantize(z_g, "zq")
        deal_w4(0, 3, 4)
        deal_w4(1, 0, PACK)

        out_rows = out.rearrange("(b p i) c -> b i p c", p=P, i=PACK)
        for g in range(N // P):
            acc = psum.tile([P, BANK], F32, name="y")
            cols = slice(P * g, P * (g + 1))
            nc.tensor.matmul_mx(
                out=acc[:],
                lhsT=w4_w[:, cols].bitcast(FP8X4),
                lhsT_scale=w4_s[:, cols],
                rhs=z_c[:].bitcast(FP8X4),
                rhs_scale=z_s[:],
                start=True,
                stop=True,
            )
            mag = work.tile([P, PICK], F32, name="mag")
            nc.scalar.activation(mag[:], acc[:], ACT.Abs)
            y = work.tile([P, PICK], F32, name="ysb")
            nc.scalar.activation(y[:], mag[:], ACT.Exp, scale=-1.0)
            page = pages[g % PAGES]
            nc.vector.tensor_tensor(page[:].indirect(list3[:]), y[:], wgo_sb[:], ALU.mult)
            nc.sync.dma_start(out_rows[g // PACK, g % PACK], page[:])
